import numpy as np
import ml_dtypes


def mxq(x, axis, fmt="e4m3"):
    dtype, down = {"e4m3": (ml_dtypes.float8_e4m3fn, 7), "e5m2": (ml_dtypes.float8_e5m2, 14)}[fmt]
    v = np.moveaxis(np.asarray(x, np.float32).astype(ml_dtypes.bfloat16).astype(np.float64), axis, -1)
    blocks = v.reshape(v.shape[:-1] + (-1, 32))
    amax = np.abs(blocks).max(-1, keepdims=True)
    byte = np.maximum(np.where(amax > 0, np.frexp(amax)[1] - 1 + 127, 0) - down, 1)
    scale = np.exp2(byte - 127.0)
    codes = (blocks / scale).astype(np.float32).astype(dtype).astype(np.float64)
    return np.moveaxis((codes * scale).reshape(v.shape), -1, axis)


WIDE = False


def mx_kscale(k):
    if not WIDE:
        return np.ones(k)
    levels = np.array([10, -10, 5, -5, 0])
    if k % 512:
        return np.exp2(np.random.permutation(np.resize(levels, k // 32))).repeat(32)
    a = np.empty((k // 512, 16))
    for p in range(k // 512):
        a[p, :8] = np.random.permutation(np.resize(levels, 8))
        for g in range(8):
            far = levels[np.abs(levels - a[p, g]) >= 10]
            a[p, g + 8] = far[np.random.randint(len(far))]
    return np.exp2(a.ravel()).repeat(32)


def f64(x):
    return np.asarray(x).astype(np.float64)


def striped(idx):
    return np.tile(idx.reshape(-1, 16).T, (8, 1)).astype(np.uint16)


def unstriped(offs):
    return offs[:16].T.reshape(-1).astype(np.int64)


def striped8(idx):
    return np.concatenate([x.reshape(-1, 16).T for x in idx]).astype(np.uint16)


def runs(offs, k):
    lists = np.stack([offs[16 * r : 16 * r + 16].T.reshape(-1) for r in range(8)]).astype(np.int64)
    return lists[np.arange(k) % 512 // 64]


def pack_weight(w):
    k, n = w.shape
    w = f64(np.asarray(w, np.float32).astype(ml_dtypes.bfloat16)).reshape(k // 32, 32, n)
    amax = np.abs(w).max(1)
    byte = np.clip(np.where(amax > 0, np.frexp(amax)[1] - 1 + 127 - 7, 1), 1, 254)
    scaled = (w * np.exp2(127.0 - byte)[:, None, :]).reshape(k, n).astype(np.float32)
    words = np.ascontiguousarray(scaled.reshape(k // 512, 128, 4, n).transpose(0, 1, 3, 2)).astype(ml_dtypes.float8_e4m3fn).view(np.uint8)
    return words, np.ascontiguousarray(byte.astype(np.uint8).reshape(k // 512, 16, n))


def unpack_weight(words, scales):
    g, p, n, _ = words.shape
    vals = np.ascontiguousarray(words).view(ml_dtypes.float8_e4m3fn).astype(np.float64) * np.repeat(np.exp2(scales.astype(np.float64) - 127.0), 8, axis=1)[..., None]
    return vals.transpose(0, 1, 3, 2).reshape(g * 512, n)


E2M1 = np.array([0.0, 0.5, 1.0, 1.5, 2.0, 3.0, 4.0, 6.0, -0.0, -0.5, -1.0, -1.5, -2.0, -3.0, -4.0, -6.0])


def pack_fp4(w):
    k, n = w.shape
    w = f64(np.asarray(w, np.float32).astype(ml_dtypes.bfloat16)).reshape(k // 32, 32, n)
    amax = np.abs(w).max(1)
    mant, ex = np.frexp(amax / 6.0)
    byte = np.clip(np.where(amax > 0, np.where(mant > 0.5, ex, ex - 1) + 127, 1), 1, 254)
    scaled = (w * np.exp2(127.0 - byte)[:, None, :]).reshape(k, n).astype(np.float32)
    c = np.ascontiguousarray(scaled.reshape(k // 512, 128, 4, n).transpose(0, 1, 3, 2)).astype(ml_dtypes.float4_e2m1fn).view(np.uint8) & 0xF
    words = (c[..., 0::2] | (c[..., 1::2] << 4)).reshape(k // 512, 128, 2 * n)
    return np.ascontiguousarray(words), np.ascontiguousarray(byte.astype(np.uint8).reshape(k // 512, 16, n))


def unpack_fp4(words, scales):
    g, _, n = scales.shape
    words = np.ascontiguousarray(words).reshape(g, 128, n, 2)
    nib = np.empty((g, 128, n, 4), np.uint8)
    nib[..., 0::2] = words & 0xF
    nib[..., 1::2] = words >> 4
    vals = E2M1[nib] * np.repeat(np.exp2(scales.astype(np.float64) - 127.0), 8, axis=1)[..., None]
    return vals.transpose(0, 1, 3, 2).reshape(g * 512, n)


def planes(y):
    n, m = y.shape
    v = y.astype(np.float32).astype(ml_dtypes.bfloat16).astype(np.float64).reshape(n // 32, 32, m)
    top = np.abs(v).max(1)
    byte = np.clip(np.where(top > 0, np.frexp(top)[1] - 1 + 127 - 7, 1), 1, 254)
    codes = (v * np.exp2(127.0 - byte)[:, None, :]).reshape(n, m).astype(np.float32).astype(ml_dtypes.float8_e4m3fn).view(np.uint8)
    words = codes.reshape(n // 512, 128, 4, m).transpose(0, 1, 3, 2)
    return np.ascontiguousarray(words), np.ascontiguousarray(byte.astype(np.uint8).reshape(n // 512, 16, m))


K, T, S, N, H, W, J, C = 512, 2048, 256, 512, 512, 192, 512, 512


def setup_inputs():
    n = np.random.standard_normal
    s = mx_kscale(K)[:, None]
    u = mx_kscale(K)
    packed_xT = pack_weight(n((K, T)) * s)
    packed_w1 = pack_fp4(n((K, H)) / np.sqrt(K) / s)
    packed_w2 = pack_fp4(n((H, N)) / np.sqrt(H) / u[:, None])
    return {
        "x_words": packed_xT[0],
        "x_scales": packed_xT[1],
        "w1_words": packed_w1[0],
        "w1_scales": packed_w1[1],
        "gn": (np.random.uniform(0.5, 1.5, (H, 1)) * u[:, None]).astype(np.float32),
        "w2_words": packed_w2[0],
        "w2_scales": packed_w2[1],
        "gs": (np.random.uniform(0.5, 1.5, (K, 1)) / s).astype(np.float32),
        "offs": striped(np.random.permutation(T)[:S]),
        "n1": striped(np.random.permutation(S)[:W]),
        "n2": striped(np.random.permutation(S)[:W]),
        "n3": striped(np.random.randint(0, S, J)),
        "cand": striped(np.random.permutation(T)[:C]),
        "n4": striped8(np.stack([np.random.permutation(S) for _ in range(8)])),
        "n5": striped8(np.stack([np.random.permutation(S) for _ in range(8)])),
    }


def reference(x_words, x_scales, w1_words, w1_scales, gn, w2_words, w2_scales, gs, offs, n1, n2, n3, cand, n4, n5):
    xq = unpack_weight(x_words, x_scales)[:, unstriped(offs)]
    y = unpack_fp4(w1_words, w1_scales).T @ xq
    pa = y[:, unstriped(n2)]
    old = y[:, unstriped(n1)]
    ra = np.maximum(pa, 0.5 * old)
    ds = y.copy()
    ds[:, unstriped(n1)] = ra
    z = f64(gn) * ds
    a = unpack_fp4(w2_words, w2_scales).T @ mxq(z, 0, "e4m3")
    x_cand = unpack_weight(x_words, x_scales)[:, unstriped(cand)]
    mb = y[:, unstriped(n3)]
    ms = mb.reshape(H, S, 2).sum(axis=2)
    mx = mb.reshape(H, S, 2).max(axis=2)
    z2 = f64(gs) * (ms - np.maximum(y, mx))
    b = 0.0625 * ((x_cand.T @ mxq(z2, 0, "e4m3")))
    out_0 = np.maximum(a, b[np.arange(C)[:, None], runs(n5, C)]) - (np.minimum(a[np.arange(N)[:, None], runs(n4, N)], b))
    return (out_0,) + planes(out_0)

@@ -1,0 +1,229 @@
+from contextlib import ExitStack
+
+import concourse.mybir as mybir
+
+K, T, S, N, H, W, J, C = 512, 2048, 256, 512, 512, 192, 512, 512
+FLOPS = 2 * K * H * S + 2 * H * N * S + 2 * K * C * S
+
+F32 = mybir.dt.float32
+BF16 = mybir.dt.bfloat16
+I32 = mybir.dt.int32
+U32 = mybir.dt.uint32
+U16 = mybir.dt.uint16
+U8 = mybir.dt.uint8
+FP8X4 = mybir.dt.float8_e4m3fn_x4
+FP4X4 = mybir.dt.float4_e2m1fn_x4
+ALU = mybir.AluOpType
+COPY = mybir.ActivationFunctionType.Copy
+
+P = 128
+PACK = 4
+Y_COLS = J + 16
+AB_COLS = 2 * S
+
+
+def tile_picked_fkcdmaxbkmaxgpair_none_po_kernel(
+    tc, x_words, x_scales, w1_words, w1_scales, gn, w2_words, w2_scales, gs, offs, n1, n2, n3, cand, n4, n5, out_0, out_1, out_2
+):
+    nc = tc.nc
+    with ExitStack() as ctx:
+        lists = ctx.enter_context(tc.tile_pool(name="lists", bufs=1))
+        sb = ctx.enter_context(tc.tile_pool(name="sb", bufs=1))
+        psum = ctx.enter_context(tc.psum_pool(name="psum", bufs=1))
+
+        def load_list(name, dram, entries):
+            held = lists.tile([P, entries // 16], U16, name=name)
+            nc.sync.dma_start(held[:], dram)
+            return held
+
+        def load_scale_rows(queue, plane, dram, quadrants):
+            for q in quadrants:
+                queue.dma_start(plane[32 * q : 32 * q + 4, :].bitcast(I32), dram[0, 4 * q : 4 * q + 4, :].bitcast(I32))
+
+        def deal_weight(name, words, scales):
+            dealt_words = sb.tile([P, 2 * H], U8, name=name + "_words", align_bytes=64)
+            dealt_scales = sb.tile([P, H], U8, name=name + "_scales", align_bytes=64)
+            nc.vector.tensor_copy(
+                dealt_words[:].rearrange("p (t m b) -> p t m b", t=PACK, b=2),
+                words.rearrange("p (m t b) -> p t m b", t=PACK, b=2),
+            )
+            nc.vector.tensor_copy(
+                dealt_scales[:].rearrange("p (t m) -> p t m", t=PACK),
+                scales.rearrange("p (m t) -> p t m", t=PACK),
+            )
+            return dealt_words, dealt_scales
+
+        x_scale_table = sb.tile([P, T], U8, align_bytes=64)
+        w1_scales_raw = sb.tile([P, H], U8, align_bytes=64)
+        w2_scales_raw = sb.tile([P, N], U8, align_bytes=64)
+        nc.vector.memset(x_scale_table[:].bitcast(I32), 0)
+        nc.gpsimd.memset(w1_scales_raw[:].bitcast(I32), 0)
+        load_scale_rows(nc.gpsimd, w1_scales_raw, w1_scales, (2, 3))
+        nc.vector.memset(w2_scales_raw[:].bitcast(I32), 0)
+        y = [sb.tile([P, Y_COLS], F32, name="y%d" % t, align_bytes=64) for t in range(PACK)]
+        for t in range(PACK):
+            nc.vector.memset(y[t][:, S:], 0.0)
+
+        offs_sb = load_list("offs_sb", offs, S)
+        n3_sb = load_list("n3_sb", n3, J)
+        w1_raw = sb.tile([P, 2 * H], U8, align_bytes=64)
+        nc.sync.dma_start(w1_raw[:].bitcast(I32), w1_words[0].bitcast(I32))
+        x_word_table = sb.tile([P, T], U32, align_bytes=64)
+        nc.sync.dma_start(x_word_table[:].bitcast(I32), x_words[0].rearrange("p n r -> p (n r)").bitcast(I32))
+        load_scale_rows(nc.sync, x_scale_table, x_scales, range(4))
+        load_scale_rows(nc.sync, w1_scales_raw, w1_scales, (0, 1))
+        cand_sb = load_list("cand_sb", cand, C)
+        gs_sb = sb.tile([P, PACK], F32)
+        nc.sync.dma_start(gs_sb[:], gs.rearrange("(p t) o -> p (t o)", t=PACK))
+        n2_sb = load_list("n2_sb", n2, W)
+        n1_sb = load_list("n1_sb", n1, W)
+        w2_raw = sb.tile([P, 2 * N], U8, align_bytes=64)
+        nc.sync.dma_start(w2_raw[:].bitcast(I32), w2_words[0].bitcast(I32))
+        load_scale_rows(nc.sync, w2_scales_raw, w2_scales, range(4))
+        gn_sb = sb.tile([P, PACK], F32)
+        nc.sync.dma_start(gn_sb[:], gn.rearrange("(p t) o -> p (t o)", t=PACK))
+        n5_sb = load_list("n5_sb", n5, S)
+        n4_sb = load_list("n4_sb", n4, S)
+
+        w1_codes, w1_plane = deal_weight("w1", w1_raw[:], w1_scales_raw[:])
+
+        picked_plane = sb.tile([P, S], U8, align_bytes=64)
+        picked_codes = sb.tile([P, S], U32, align_bytes=64)
+        cand_plane_raw = sb.tile([P, C], U8, align_bytes=64)
+        cand_plane = sb.tile([P, C], U8, align_bytes=64)
+        cand_codes = sb.tile([P, C], U32, align_bytes=64)
+        nc.vector.tensor_copy(picked_plane[:], x_scale_table[:].indirect(offs_sb[:]))
+        nc.vector.tensor_copy(picked_codes[:], x_word_table[:].indirect(offs_sb[:]))
+        nc.vector.tensor_copy(cand_plane_raw[:], x_scale_table[:].indirect(cand_sb[:]))
+        nc.vector.tensor_copy(
+            cand_plane[:].rearrange("p (t m) -> p t m", t=PACK), cand_plane_raw[:].rearrange("p (m t) -> p t m", t=PACK)
+        )
+
+        y_psum = [psum.tile([P, S], F32, name="y_psum%d" % t) for t in range(PACK)]
+        for t in range(PACK):
+            nc.tensor.matmul_mx(
+                out=y_psum[t][:],
+                lhsT=w1_codes[:, 2 * P * t : 2 * P * (t + 1)].bitcast(FP4X4),
+                lhsT_scale=w1_plane[:, P * t : P * (t + 1)],
+                rhs=picked_codes[:].bitcast(FP8X4),
+                rhs_scale=picked_plane[:],
+                start=True,
+                stop=True,
+            )
+        nc.scalar.activation(y[0][:, :S], y_psum[0][:], COPY)
+        nc.vector.tensor_copy(cand_codes[:].rearrange("p (t m) -> p m t", t=PACK), x_word_table[:].indirect(cand_sb[:]))
+        for t in range(1, PACK):
+            nc.vector.tensor_copy(y[t][:, :S], y_psum[t][:])
+
+        a_win = [sb.tile([P, AB_COLS], F32, name="a_win%d" % t, align_bytes=64) for t in range(PACK)]
+        b_win = [sb.tile([P, AB_COLS], F32, name="b_win%d" % t, align_bytes=64) for t in range(PACK)]
+        spread = sb.tile([P, PACK, S], F32, align_bytes=64)
+        for t in range(PACK):
+            members = sb.tile([P, J], F32, name="members%d" % t, align_bytes=64)
+            nc.scalar.activation(members[:], y[t][:].indirect(n3_sb[:]), COPY)
+            first = members[:, 0:J:2]
+            second = members[:, 1:J:2]
+            top = sb.tile([P, S], F32, name="top%d" % t, align_bytes=64)
+            nc.vector.tensor_tensor(top[:], y_psum[t][:], first, ALU.max)
+            gap = b_win[t][:, S:]
+            nc.vector.tensor_tensor(gap, second, top[:], ALU.subtract)
+            nc.vector.scalar_tensor_tensor(spread[:, t, :], gap, 0.0, first, ALU.min, ALU.add)
+
+        z2_bf = sb.tile([P, S * PACK], BF16, align_bytes=64)
+        nc.vector.tensor_tensor(
+            z2_bf[:].rearrange("p (c i t) -> p c t i", i=4, t=PACK),
+            spread[:].rearrange("p t (c i) -> p c t i", i=4),
+            gs_sb[:].rearrange("p (c t i) -> p c t i", c=1, i=1).to_broadcast([P, S // 4, PACK, 4]),
+            ALU.mult,
+        )
+        z2_codes = sb.tile([P, S], U32, align_bytes=64)
+        z2_plane = sb.tile([P, S], U8, align_bytes=64)
+        nc.vector.quantize_mx(out=z2_codes[:].bitcast(FP8X4), scales=z2_plane[:], in_=z2_bf[:])
+        b_psum = [psum.tile([P, 2, S], F32, name="b_psum%d" % u) for u in range(2)]
+        for t in range(PACK):
+            nc.tensor.matmul_mx(
+                out=b_psum[t // 2][:, t % 2, :],
+                lhsT=cand_codes[:, P * t : P * (t + 1)].bitcast(FP8X4),
+                lhsT_scale=cand_plane[:, P * t : P * (t + 1)],
+                rhs=z2_codes[:].bitcast(FP8X4),
+                rhs_scale=z2_plane[:],
+                start=True,
+                stop=True,
+            )
+
+        w2_codes, w2_plane = deal_weight("w2", w2_raw[:], w2_scales_raw[:])
+
+        z_bf = sb.tile([P, S, PACK], BF16, align_bytes=64)
+        taken = []
+
+        def fetch(t):
+            pa = sb.tile([P, W], F32, name="pa%d" % t, align_bytes=64)
+            old = sb.tile([P, W], F32, name="old%d" % t, align_bytes=64)
+            ra = sb.tile([P, W], F32, name="ra%d" % t, align_bytes=64)
+            nc.scalar.activation(pa[:], y[t][:].indirect(n2_sb[:]), COPY)
+            nc.scalar.activation(old[:], y[t][:].indirect(n1_sb[:]), COPY)
+            nc.vector.scalar_tensor_tensor(ra[:], old[:], 0.5, pa[:], ALU.mult, ALU.max)
+            taken.append(ra)
+
+        def put(t):
+            nc.scalar.activation(y[t][:].indirect(n1_sb[:]), taken[t][:], COPY)
+            nc.vector.tensor_scalar(z_bf[:, :, t], y[t][:, :S], gn_sb[:, t : t + 1], None, ALU.mult)
+
+        fetch(0)
+        for t in range(1, PACK):
+            fetch(t)
+            put(t - 1)
+            if t == 1:
+                for u in range(PACK):
+                    nc.vector.tensor_scalar(b_win[u][:, :S], b_psum[u // 2][:, u % 2, :], 0.0625, None, ALU.mult)
+        put(PACK - 1)
+
+        z_codes = sb.tile([P, S], U32, align_bytes=64)
+        z_plane = sb.tile([P, S], U8, align_bytes=64)
+        nc.vector.quantize_mx(out=z_codes[:].bitcast(FP8X4), scales=z_plane[:], in_=z_bf[:].rearrange("p j t -> p (j t)"))
+        a_psum = [psum.tile([P, 2, S], F32, name="a_psum%d" % u) for u in range(2)]
+        for t in range(PACK):
+            nc.tensor.matmul_mx(
+                out=a_psum[t // 2][:, t % 2, :],
+                lhsT=w2_codes[:, 2 * P * t : 2 * P * (t + 1)].bitcast(FP4X4),
+                lhsT_scale=w2_plane[:, P * t : P * (t + 1)],
+                rhs=z_codes[:].bitcast(FP8X4),
+                rhs_scale=z_plane[:],
+                start=True,
+                stop=True,
+            )
+
+        for t in range(PACK):
+            nc.scalar.activation(a_win[t][:, S:], b_win[t][:].indirect(n5_sb[:]), COPY)
+        for t in range(2):
+            nc.vector.tensor_copy(a_win[t][:, :S], a_psum[0][:, t, :])
+
+        result = sb.tile([P, PACK, S], F32, align_bytes=64)
+        result_bf = sb.tile([P, S, PACK], BF16, align_bytes=64)
+        out_rows = out_0.rearrange("(p t) j -> p t j", t=PACK)
+        upper = []
+        for t in range(PACK):
+            high = sb.tile([P, S], F32, name="high%d" % t, align_bytes=64)
+            nc.vector.tensor_tensor(high[:], a_psum[t // 2][:, t % 2, :], a_win[t][:, S:], ALU.max)
+            upper.append(high)
+        for t in range(PACK):
+            a_at = sb.tile([P, S], F32, name="a_at%d" % t, align_bytes=64)
+            low = sb.tile([P, S], F32, name="low%d" % t, align_bytes=64)
+            if t >= 2:
+                nc.scalar.activation(a_win[t][:, :S], a_psum[1][:, t % 2, :], COPY)
+            nc.scalar.activation(a_at[:], a_win[t][:].indirect(n4_sb[:]), COPY)
+            nc.vector.tensor_tensor(low[:], a_at[:], b_win[t][:, :S], ALU.min)
+            nc.vector.tensor_tensor(result[:, t, :], upper[t][:], low[:], ALU.subtract)
+            nc.sync.dma_start(out_rows[:, t, :], result[:, t, :])
+        nc.scalar.copy(result_bf[:, :, 0:2], result[:, 0:2, :].rearrange("p t j -> p j t"))
+        nc.vector.tensor_copy(result_bf[:, :, 2:4], result[:, 2:4, :].rearrange("p t j -> p j t"))
+
+        out_codes = sb.tile([P, S], U32, align_bytes=64)
+        out_plane = sb.tile([P, S], U8, align_bytes=64)
+        nc.vector.quantize_mx(
+            out=out_codes[:].bitcast(FP8X4), scales=out_plane[:], in_=result_bf[:].rearrange("p j t -> p (j t)")
+        )
+        nc.sync.dma_start(out_1[0].rearrange("p n r -> p (n r)").bitcast(I32), out_codes[:].bitcast(I32))
+        for q in range(4):
+            queue = nc.scalar if q % 2 == 0 else nc.sync
+            queue.dma_start(out_2[0, 4 * q : 4 * q + 4, :].bitcast(I32), out_plane[32 * q : 32 * q + 4, :].bitcast(I32))

@@ -40,38 +40,49 @@ def tile_picked_fkcdmaxbkmaxgpair_none_po_kernel(
             for q in quadrants:
                 queue.dma_start(plane[32 * q : 32 * q + 4, :].bitcast(I32), dram[0, 4 * q : 4 * q + 4, :].bitcast(I32))
 
-        def deal_weight(name, words, scales):
-            dealt_words = sb.tile([P, 2 * H], U8, name=name + "_words", align_bytes=64)
-            dealt_scales = sb.tile([P, H], U8, name=name + "_scales", align_bytes=64)
+        def deal_words(name, words):
+            dealt = sb.tile([P, 2 * H], U8, name=name, align_bytes=64)
             nc.vector.tensor_copy(
-                dealt_words[:].rearrange("p (t m b) -> p t m b", t=PACK, b=2),
-                words.rearrange("p (m t b) -> p t m b", t=PACK, b=2),
+                dealt[:].rearrange("p (t m b) -> p t m b", t=PACK, b=2),
+                words[:].rearrange("p (m t b) -> p t m b", t=PACK, b=2),
             )
+            return dealt
+
+        def deal_scales(name, scales):
+            dealt = sb.tile([P, H], U8, name=name, align_bytes=64)
             nc.vector.tensor_copy(
-                dealt_scales[:].rearrange("p (t m) -> p t m", t=PACK),
-                scales.rearrange("p (m t) -> p t m", t=PACK),
+                dealt[:].rearrange("p (t m) -> p t m", t=PACK), scales[:].rearrange("p (m t) -> p t m", t=PACK)
             )
-            return dealt_words, dealt_scales
+            return dealt
+
+        def quantise(name, values):
+            codes = sb.tile([P, S], U32, name=name + "_codes", align_bytes=64)
+            plane = sb.tile([P, S], U8, name=name + "_plane", align_bytes=64)
+            nc.vector.quantize_mx(out=codes[:].bitcast(FP8X4), scales=plane[:], in_=values[:].rearrange("p j t -> p (j t)"))
+            return codes, plane
+
+        def planes(name, cols):
+            return [sb.tile([P, cols], F32, name="%s%d" % (name, t), align_bytes=64) for t in range(PACK)]
 
         x_scale_table = sb.tile([P, T], U8, align_bytes=64)
         w1_scales_raw = sb.tile([P, H], U8, align_bytes=64)
         w2_scales_raw = sb.tile([P, N], U8, align_bytes=64)
-        nc.vector.memset(x_scale_table[:].bitcast(I32), 0)
-        nc.gpsimd.memset(w1_scales_raw[:].bitcast(I32), 0)
-        load_scale_rows(nc.gpsimd, w1_scales_raw, w1_scales, (2, 3))
+        nc.vector.memset(x_scale_table[:, : T // 2].bitcast(I32), 0)
+        nc.gpsimd.memset(x_scale_table[:, T // 2 :].bitcast(I32), 0)
+        nc.vector.memset(w1_scales_raw[:].bitcast(I32), 0)
         nc.vector.memset(w2_scales_raw[:].bitcast(I32), 0)
         y = [sb.tile([P, Y_COLS], F32, name="y%d" % t, align_bytes=64) for t in range(PACK)]
         for t in range(PACK):
             nc.vector.memset(y[t][:, S:], 0.0)
 
         offs_sb = load_list("offs_sb", offs, S)
-        n3_sb = load_list("n3_sb", n3, J)
         w1_raw = sb.tile([P, 2 * H], U8, align_bytes=64)
         nc.sync.dma_start(w1_raw[:].bitcast(I32), w1_words[0].bitcast(I32))
+        n3_sb = load_list("n3_sb", n3, J)
+        load_scale_rows(nc.sync, x_scale_table, x_scales, range(4))
         x_word_table = sb.tile([P, T], U32, align_bytes=64)
         nc.sync.dma_start(x_word_table[:].bitcast(I32), x_words[0].rearrange("p n r -> p (n r)").bitcast(I32))
-        load_scale_rows(nc.sync, x_scale_table, x_scales, range(4))
-        load_scale_rows(nc.sync, w1_scales_raw, w1_scales, (0, 1))
+        load_scale_rows(nc.sync, w1_scales_raw, w1_scales, range(4))
         cand_sb = load_list("cand_sb", cand, C)
         gs_sb = sb.tile([P, PACK], F32)
         nc.sync.dma_start(gs_sb[:], gs.rearrange("(p t) o -> p (t o)", t=PACK))
@@ -85,18 +96,17 @@ def tile_picked_fkcdmaxbkmaxgpair_none_po_kernel(
         n5_sb = load_list("n5_sb", n5, S)
         n4_sb = load_list("n4_sb", n4, S)
 
-        w1_codes, w1_plane = deal_weight("w1", w1_raw[:], w1_scales_raw[:])
-
         picked_plane = sb.tile([P, S], U8, align_bytes=64)
-        picked_codes = sb.tile([P, S], U32, align_bytes=64)
+        picked_codes = sb.tile([P, S], U32, tag="gathered_words", align_bytes=64)
         cand_plane_raw = sb.tile([P, C], U8, align_bytes=64)
-        cand_plane = sb.tile([P, C], U8, align_bytes=64)
-        cand_codes = sb.tile([P, C], U32, align_bytes=64)
+        w1_codes = deal_words("w1_codes", w1_raw)
         nc.vector.tensor_copy(picked_plane[:], x_scale_table[:].indirect(offs_sb[:]))
         nc.vector.tensor_copy(picked_codes[:], x_word_table[:].indirect(offs_sb[:]))
-        nc.vector.tensor_copy(cand_plane_raw[:], x_scale_table[:].indirect(cand_sb[:]))
+        w1_plane = sb.tile([P, H], U8, align_bytes=64)
+        nc.vector.tensor_copy(w1_plane[:, :P], w1_scales_raw[:, 0:H:PACK])
         nc.vector.tensor_copy(
-            cand_plane[:].rearrange("p (t m) -> p t m", t=PACK), cand_plane_raw[:].rearrange("p (m t) -> p t m", t=PACK)
+            w1_plane[:, P:].rearrange("p (t m) -> p t m", t=PACK - 1),
+            w1_scales_raw[:].rearrange("p (m t) -> p t m", t=PACK)[:, 1:, :],
         )
 
         y_psum = [psum.tile([P, S], F32, name="y_psum%d" % t) for t in range(PACK)]
@@ -110,35 +120,83 @@ def tile_picked_fkcdmaxbkmaxgpair_none_po_kernel(
                 start=True,
                 stop=True,
             )
-        nc.scalar.activation(y[0][:, :S], y_psum[0][:], COPY)
-        nc.vector.tensor_copy(cand_codes[:].rearrange("p (t m) -> p m t", t=PACK), x_word_table[:].indirect(cand_sb[:]))
-        for t in range(1, PACK):
+
+        a_win = planes("a_win", AB_COLS)
+        b_win = planes("b_win", AB_COLS)
+        members = planes("members", J)
+        top = planes("top", S)
+        spread = sb.tile([P, PACK, S], F32, align_bytes=64)
+        pa = sb.tile([P, PACK, W], F32, align_bytes=64)
+        old = sb.tile([P, PACK, W], F32, align_bytes=64)
+        ra = sb.tile([P, PACK, W], F32, align_bytes=64)
+        z_bf = sb.tile([P, S, PACK], BF16, align_bytes=64)
+        z2_bf = sb.tile([P, S, PACK], BF16, align_bytes=64)
+
+        def copy_y(t):
             nc.vector.tensor_copy(y[t][:, :S], y_psum[t][:])
 
-        a_win = [sb.tile([P, AB_COLS], F32, name="a_win%d" % t, align_bytes=64) for t in range(PACK)]
-        b_win = [sb.tile([P, AB_COLS], F32, name="b_win%d" % t, align_bytes=64) for t in range(PACK)]
-        spread = sb.tile([P, PACK, S], F32, align_bytes=64)
-        for t in range(PACK):
-            members = sb.tile([P, J], F32, name="members%d" % t, align_bytes=64)
-            nc.scalar.activation(members[:], y[t][:].indirect(n3_sb[:]), COPY)
-            first = members[:, 0:J:2]
-            second = members[:, 1:J:2]
-            top = sb.tile([P, S], F32, name="top%d" % t, align_bytes=64)
-            nc.vector.tensor_tensor(top[:], y_psum[t][:], first, ALU.max)
-            gap = b_win[t][:, S:]
-            nc.vector.tensor_tensor(gap, second, top[:], ALU.subtract)
-            nc.vector.scalar_tensor_tensor(spread[:, t, :], gap, 0.0, first, ALU.min, ALU.add)
+        def fetch_members(t):
+            nc.scalar.activation(members[t][:], y[t][:].indirect(n3_sb[:]), COPY)
 
-        z2_bf = sb.tile([P, S * PACK], BF16, align_bytes=64)
+        def take_top(t):
+            nc.vector.tensor_tensor(top[t][:], y_psum[t][:], members[t][:, 0:J:2], ALU.max)
+
+        def take_gap(t):
+            nc.vector.tensor_tensor(b_win[t][:, S:], members[t][:, 1:J:2], top[t][:], ALU.subtract)
+
+        def take_spread(t):
+            nc.vector.scalar_tensor_tensor(spread[:, t, :], b_win[t][:, S:], 0.0, members[t][:, 0:J:2], ALU.min, ALU.add)
+
+        def fetch_pair(t):
+            nc.scalar.activation(pa[:, t, :], y[t][:].indirect(n2_sb[:]), COPY)
+            nc.scalar.activation(old[:, t, :], y[t][:].indirect(n1_sb[:]), COPY)
+
+        def take_ra(u):
+            two = slice(2 * u, 2 * u + 2)
+            nc.vector.scalar_tensor_tensor(ra[:, two, :], old[:, two, :], 0.5, pa[:, two, :], ALU.mult, ALU.max)
+
+        def put(t):
+            nc.scalar.activation(y[t][:].indirect(n1_sb[:]), ra[:, t, :], COPY)
+
+        def round_z(t):
+            nc.vector.tensor_scalar(z_bf[:, :, t], y[t][:, :S], gn_sb[:, t : t + 1], None, ALU.mult)
+
+        nc.scalar.activation(y[0][:, :S], y_psum[0][:], COPY)
+        fetch_members(0)
+        for t in range(1, PACK):
+            copy_y(t)
+            fetch_members(t)
+        for t in range(PACK):
+            fetch_pair(t)
+        nc.vector.tensor_copy(cand_plane_raw[:], x_scale_table[:].indirect(cand_sb[:]))
+        take_top(0)
+        cand_plane = deal_scales("cand_plane", cand_plane_raw)
+        take_gap(0)
+        take_top(1)
+        take_spread(0)
+        take_gap(1)
+        take_top(2)
+        take_spread(1)
+        take_gap(2)
+        w2_codes = deal_words("w2_codes", w2_raw)
+        take_top(3)
+        take_spread(2)
+        take_gap(3)
+        w2_plane = deal_scales("w2_plane", w2_scales_raw)
+        take_spread(3)
+        take_ra(0)
         nc.vector.tensor_tensor(
-            z2_bf[:].rearrange("p (c i t) -> p c t i", i=4, t=PACK),
+            z2_bf[:].rearrange("p (c i) t -> p c t i", i=4),
             spread[:].rearrange("p t (c i) -> p c t i", i=4),
             gs_sb[:].rearrange("p (c t i) -> p c t i", c=1, i=1).to_broadcast([P, S // 4, PACK, 4]),
             ALU.mult,
         )
-        z2_codes = sb.tile([P, S], U32, align_bytes=64)
-        z2_plane = sb.tile([P, S], U8, align_bytes=64)
-        nc.vector.quantize_mx(out=z2_codes[:].bitcast(FP8X4), scales=z2_plane[:], in_=z2_bf[:])
+        take_ra(1)
+        for t in range(PACK):
+            put(t)
+        z2_codes, z2_plane = quantise("z2", z2_bf)
+        cand_codes = sb.tile([P, C], U32, tag="gathered_words", align_bytes=64)
+        nc.vector.tensor_copy(cand_codes[:].rearrange("p (t m) -> p m t", t=PACK), x_word_table[:].indirect(cand_sb[:]))
         b_psum = [psum.tile([P, 2, S], F32, name="b_psum%d" % u) for u in range(2)]
         for t in range(PACK):
             nc.tensor.matmul_mx(
@@ -150,37 +208,13 @@ def tile_picked_fkcdmaxbkmaxgpair_none_po_kernel(
                 start=True,
                 stop=True,
             )
-
-        w2_codes, w2_plane = deal_weight("w2", w2_raw[:], w2_scales_raw[:])
-
-        z_bf = sb.tile([P, S, PACK], BF16, align_bytes=64)
-        taken = []
-
-        def fetch(t):
-            pa = sb.tile([P, W], F32, name="pa%d" % t, align_bytes=64)
-            old = sb.tile([P, W], F32, name="old%d" % t, align_bytes=64)
-            ra = sb.tile([P, W], F32, name="ra%d" % t, align_bytes=64)
-            nc.scalar.activation(pa[:], y[t][:].indirect(n2_sb[:]), COPY)
-            nc.scalar.activation(old[:], y[t][:].indirect(n1_sb[:]), COPY)
-            nc.vector.scalar_tensor_tensor(ra[:], old[:], 0.5, pa[:], ALU.mult, ALU.max)
-            taken.append(ra)
-
-        def put(t):
-            nc.scalar.activation(y[t][:].indirect(n1_sb[:]), taken[t][:], COPY)
-            nc.vector.tensor_scalar(z_bf[:, :, t], y[t][:, :S], gn_sb[:, t : t + 1], None, ALU.mult)
-
-        fetch(0)
-        for t in range(1, PACK):
-            fetch(t)
-            put(t - 1)
-            if t == 1:
-                for u in range(PACK):
-                    nc.vector.tensor_scalar(b_win[u][:, :S], b_psum[u // 2][:, u % 2, :], 0.0625, None, ALU.mult)
-        put(PACK - 1)
-
-        z_codes = sb.tile([P, S], U32, align_bytes=64)
-        z_plane = sb.tile([P, S], U8, align_bytes=64)
-        nc.vector.quantize_mx(out=z_codes[:].bitcast(FP8X4), scales=z_plane[:], in_=z_bf[:].rearrange("p j t -> p (j t)"))
+        round_z(0)
+        round_z(1)
+        for t in range(PACK):
+            nc.vector.tensor_scalar(b_win[t][:, :S], b_psum[t // 2][:, t % 2, :], 0.0625, None, ALU.mult)
+        round_z(2)
+        round_z(3)
+        z_codes, z_plane = quantise("z", z_bf)
         a_psum = [psum.tile([P, 2, S], F32, name="a_psum%d" % u) for u in range(2)]
         for t in range(PACK):
             nc.tensor.matmul_mx(
@@ -201,28 +235,40 @@ def tile_picked_fkcdmaxbkmaxgpair_none_po_kernel(
         result = sb.tile([P, PACK, S], F32, align_bytes=64)
         result_bf = sb.tile([P, S, PACK], BF16, align_bytes=64)
         out_rows = out_0.rearrange("(p t) j -> p t j", t=PACK)
-        upper = []
+        high = planes("high", S)
+        low = planes("low", S)
+        a_at = planes("a_at", S)
+
+        def take_high(t):
+            nc.vector.tensor_tensor(high[t][:], a_psum[t // 2][:, t % 2, :], a_win[t][:, S:], ALU.max)
+
+        def take_low(t):
+            nc.vector.tensor_tensor(low[t][:], a_at[t][:], b_win[t][:, :S], ALU.min)
+
+        def take_result(t):
+            nc.vector.tensor_tensor(result[:, t, :], high[t][:], low[t][:], ALU.subtract)
+            nc.sync.dma_start(out_rows[:, t, :], result[:, t, :])
+
         for t in range(PACK):
-            high = sb.tile([P, S], F32, name="high%d" % t, align_bytes=64)
-            nc.vector.tensor_tensor(high[:], a_psum[t // 2][:, t % 2, :], a_win[t][:, S:], ALU.max)
-            upper.append(high)
-        for t in range(PACK):
-            a_at = sb.tile([P, S], F32, name="a_at%d" % t, align_bytes=64)
-            low = sb.tile([P, S], F32, name="low%d" % t, align_bytes=64)
             if t >= 2:
                 nc.scalar.activation(a_win[t][:, :S], a_psum[1][:, t % 2, :], COPY)
-            nc.scalar.activation(a_at[:], a_win[t][:].indirect(n4_sb[:]), COPY)
-            nc.vector.tensor_tensor(low[:], a_at[:], b_win[t][:, :S], ALU.min)
-            nc.vector.tensor_tensor(result[:, t, :], upper[t][:], low[:], ALU.subtract)
-            nc.sync.dma_start(out_rows[:, t, :], result[:, t, :])
+            nc.scalar.activation(a_at[t][:], a_win[t][:].indirect(n4_sb[:]), COPY)
+        take_high(0)
+        take_high(1)
+        take_low(0)
+        take_high(2)
+        take_low(1)
+        take_result(0)
+        take_high(3)
+        take_result(1)
         nc.scalar.copy(result_bf[:, :, 0:2], result[:, 0:2, :].rearrange("p t j -> p j t"))
+        take_low(2)
+        take_low(3)
+        take_result(2)
+        take_result(3)
         nc.vector.tensor_copy(result_bf[:, :, 2:4], result[:, 2:4, :].rearrange("p t j -> p j t"))
 
-        out_codes = sb.tile([P, S], U32, align_bytes=64)
-        out_plane = sb.tile([P, S], U8, align_bytes=64)
-        nc.vector.quantize_mx(
-            out=out_codes[:].bitcast(FP8X4), scales=out_plane[:], in_=result_bf[:].rearrange("p j t -> p (j t)")
-        )
+        out_codes, out_plane = quantise("out", result_bf)
         nc.sync.dma_start(out_1[0].rearrange("p n r -> p (n r)").bitcast(I32), out_codes[:].bitcast(I32))
         for q in range(4):
             queue = nc.scalar if q % 2 == 0 else nc.sync

@@ -109,7 +109,7 @@ def tile_picked_fkcdmaxbkmaxgpair_none_po_kernel(
             w1_scales_raw[:].rearrange("p (m t) -> p t m", t=PACK)[:, 1:, :],
         )
 
-        y_psum = [psum.tile([P, S], F32, name="y_psum%d" % t) for t in range(PACK)]
+        y_psum = [psum.tile([P, S], F32, name="y_psum%d" % t, tag="ya%d" % t) for t in range(PACK)]
         for t in range(PACK):
             nc.tensor.matmul_mx(
                 out=y_psum[t][:],
@@ -131,6 +131,9 @@ def tile_picked_fkcdmaxbkmaxgpair_none_po_kernel(
         ra = sb.tile([P, PACK, W], F32, align_bytes=64)
         z_bf = sb.tile([P, S, PACK], BF16, align_bytes=64)
         z2_bf = sb.tile([P, S, PACK], BF16, align_bytes=64)
+
+        whole = slice(0, S)
+        halves = (slice(0, S // 2), slice(S // 2, S))
 
         def copy_y(t):
             nc.vector.tensor_copy(y[t][:, :S], y_psum[t][:])
@@ -158,8 +161,8 @@ def tile_picked_fkcdmaxbkmaxgpair_none_po_kernel(
         def put(t):
             nc.scalar.activation(y[t][:].indirect(n1_sb[:]), ra[:, t, :], COPY)
 
-        def round_z(t):
-            nc.vector.tensor_scalar(z_bf[:, :, t], y[t][:, :S], gn_sb[:, t : t + 1], None, ALU.mult)
+        def round_z(t, cols):
+            nc.vector.tensor_scalar(z_bf[:, cols, t], y[t][:, cols], gn_sb[:, t : t + 1], None, ALU.mult)
 
         nc.scalar.activation(y[0][:, :S], y_psum[0][:], COPY)
         fetch_members(0)
@@ -197,10 +200,10 @@ def tile_picked_fkcdmaxbkmaxgpair_none_po_kernel(
         z2_codes, z2_plane = quantise("z2", z2_bf)
         cand_codes = sb.tile([P, C], U32, tag="gathered_words", align_bytes=64)
         nc.vector.tensor_copy(cand_codes[:].rearrange("p (t m) -> p m t", t=PACK), x_word_table[:].indirect(cand_sb[:]))
-        b_psum = [psum.tile([P, 2, S], F32, name="b_psum%d" % u) for u in range(2)]
+        b_psum = [psum.tile([P, S], F32, name="b_psum%d" % t) for t in range(PACK)]
         for t in range(PACK):
             nc.tensor.matmul_mx(
-                out=b_psum[t // 2][:, t % 2, :],
+                out=b_psum[t][:],
                 lhsT=cand_codes[:, P * t : P * (t + 1)].bitcast(FP8X4),
                 lhsT_scale=cand_plane[:, P * t : P * (t + 1)],
                 rhs=z2_codes[:].bitcast(FP8X4),
@@ -208,17 +211,25 @@ def tile_picked_fkcdmaxbkmaxgpair_none_po_kernel(
                 start=True,
                 stop=True,
             )
-        round_z(0)
-        round_z(1)
+        round_z(0, whole)
+        round_z(1, whole)
         for t in range(PACK):
-            nc.vector.tensor_scalar(b_win[t][:, :S], b_psum[t // 2][:, t % 2, :], 0.0625, None, ALU.mult)
-        round_z(2)
-        round_z(3)
-        z_codes, z_plane = quantise("z", z_bf)
-        a_psum = [psum.tile([P, 2, S], F32, name="a_psum%d" % u) for u in range(2)]
+            nc.vector.tensor_scalar(b_win[t][:, :S], b_psum[t][:], 0.0625, None, ALU.mult)
+        round_z(2, whole)
+        z_codes = sb.tile([P, S], U32, align_bytes=64)
+        z_plane = sb.tile([P, S], U8, align_bytes=64)
+        for cols in halves:
+            round_z(3, cols)
+        for cols in halves:
+            nc.vector.quantize_mx(
+                out=z_codes[:, cols].bitcast(FP8X4),
+                scales=z_plane[:, cols],
+                in_=z_bf[:, cols, :].rearrange("p j t -> p (j t)"),
+            )
+        a_psum = [psum.tile([P, S], F32, name="a_psum%d" % t, tag="ya%d" % t) for t in range(PACK)]
         for t in range(PACK):
             nc.tensor.matmul_mx(
-                out=a_psum[t // 2][:, t % 2, :],
+                out=a_psum[t][:],
                 lhsT=w2_codes[:, 2 * P * t : 2 * P * (t + 1)].bitcast(FP4X4),
                 lhsT_scale=w2_plane[:, P * t : P * (t + 1)],
                 rhs=z_codes[:].bitcast(FP8X4),
@@ -229,8 +240,8 @@ def tile_picked_fkcdmaxbkmaxgpair_none_po_kernel(
 
         for t in range(PACK):
             nc.scalar.activation(a_win[t][:, S:], b_win[t][:].indirect(n5_sb[:]), COPY)
-        for t in range(2):
-            nc.vector.tensor_copy(a_win[t][:, :S], a_psum[0][:, t, :])
+        for t in range(PACK):
+            nc.vector.tensor_copy(a_win[t][:, :S], a_psum[t][:])
 
         result = sb.tile([P, PACK, S], F32, align_bytes=64)
         result_bf = sb.tile([P, S, PACK], BF16, align_bytes=64)
@@ -239,36 +250,58 @@ def tile_picked_fkcdmaxbkmaxgpair_none_po_kernel(
         low = planes("low", S)
         a_at = planes("a_at", S)
 
+        out_codes = sb.tile([P, S], U32, align_bytes=64)
+        out_plane = sb.tile([P, S], U8, align_bytes=64)
+
+        def fetch_a(t, cols):
+            nc.scalar.activation(a_at[t][:, cols], a_win[t][:].indirect(n4_sb[:, cols.start // 16 : cols.stop // 16]), COPY)
+
         def take_high(t):
-            nc.vector.tensor_tensor(high[t][:], a_psum[t // 2][:, t % 2, :], a_win[t][:, S:], ALU.max)
+            nc.vector.tensor_tensor(high[t][:], a_psum[t][:], a_win[t][:, S:], ALU.max)
 
-        def take_low(t):
-            nc.vector.tensor_tensor(low[t][:], a_at[t][:], b_win[t][:, :S], ALU.min)
+        def take_low(t, cols):
+            nc.vector.scalar_tensor_tensor(low[t][:, cols], b_psum[t][:, cols], 0.0625, a_at[t][:, cols], ALU.mult, ALU.min)
 
-        def take_result(t):
-            nc.vector.tensor_tensor(result[:, t, :], high[t][:], low[t][:], ALU.subtract)
-            nc.sync.dma_start(out_rows[:, t, :], result[:, t, :])
+        def take_result(engine, t, cols):
+            engine.tensor_tensor(result[:, t, cols], high[t][:, cols], low[t][:, cols], ALU.subtract)
 
-        for t in range(PACK):
-            if t >= 2:
-                nc.scalar.activation(a_win[t][:, :S], a_psum[1][:, t % 2, :], COPY)
-            nc.scalar.activation(a_at[t][:], a_win[t][:].indirect(n4_sb[:]), COPY)
+        def round_result(cols):
+            nc.vector.tensor_copy(
+                result_bf[:, cols, :].rearrange("p (c i) t -> p c t i", i=4),
+                result[:, :, cols].rearrange("p t (c i) -> p c t i", i=4),
+            )
+
+        def quantise_result(cols):
+            nc.vector.quantize_mx(
+                out=out_codes[:, cols].bitcast(FP8X4),
+                scales=out_plane[:, cols],
+                in_=result_bf[:, cols, :].rearrange("p j t -> p (j t)"),
+            )
+
+        for t in range(PACK - 1):
+            fetch_a(t, whole)
+        for cols in halves:
+            fetch_a(PACK - 1, cols)
         take_high(0)
         take_high(1)
-        take_low(0)
+        take_low(0, whole)
         take_high(2)
-        take_low(1)
-        take_result(0)
+        take_low(1, whole)
+        take_result(nc.gpsimd, 0, whole)
         take_high(3)
-        take_result(1)
-        nc.scalar.copy(result_bf[:, :, 0:2], result[:, 0:2, :].rearrange("p t j -> p j t"))
-        take_low(2)
-        take_low(3)
-        take_result(2)
-        take_result(3)
-        nc.vector.tensor_copy(result_bf[:, :, 2:4], result[:, 2:4, :].rearrange("p t j -> p j t"))
-
-        out_codes, out_plane = quantise("out", result_bf)
+        take_result(nc.gpsimd, 1, whole)
+        nc.sync.dma_start(out_rows[:, 0:2, :], result[:, 0:2, :])
+        take_low(2, whole)
+        for cols in halves:
+            take_low(3, cols)
+        take_result(nc.vector, 2, whole)
+        for cols in halves:
+            take_result(nc.vector, 3, cols)
+        nc.sync.dma_start(out_rows[:, 2:4, :], result[:, 2:4, :])
+        for cols in halves:
+            round_result(cols)
+        for cols in halves:
+            quantise_result(cols)
         nc.sync.dma_start(out_1[0].rearrange("p n r -> p (n r)").bitcast(I32), out_codes[:].bitcast(I32))
         for q in range(4):
             queue = nc.scalar if q % 2 == 0 else nc.sync

@@ -48,8 +48,8 @@ def tile_picked_fkcdmaxbkmaxgpair_none_po_kernel(
             )
             return dealt
 
-        def deal_scales(name, scales):
-            dealt = sb.tile([P, H], U8, name=name, align_bytes=64)
+        def deal_scales(name, scales, tag):
+            dealt = sb.tile([P, H], U8, name=name, tag=tag, align_bytes=64)
             nc.vector.tensor_copy(
                 dealt[:].rearrange("p (t m) -> p t m", t=PACK), scales[:].rearrange("p (m t) -> p t m", t=PACK)
             )
@@ -65,7 +65,7 @@ def tile_picked_fkcdmaxbkmaxgpair_none_po_kernel(
             return [sb.tile([P, cols], F32, name="%s%d" % (name, t), align_bytes=64) for t in range(PACK)]
 
         x_scale_table = sb.tile([P, T], U8, align_bytes=64)
-        w1_scales_raw = sb.tile([P, H], U8, align_bytes=64)
+        w1_scales_raw = sb.tile([P, H], U8, tag="scale_rows", align_bytes=64)
         w2_scales_raw = sb.tile([P, N], U8, align_bytes=64)
         nc.vector.memset(x_scale_table[:, : T // 2].bitcast(I32), 0)
         nc.gpsimd.memset(x_scale_table[:, T // 2 :].bitcast(I32), 0)
@@ -78,18 +78,18 @@ def tile_picked_fkcdmaxbkmaxgpair_none_po_kernel(
         offs_sb = load_list("offs_sb", offs, S)
         w1_raw = sb.tile([P, 2 * H], U8, align_bytes=64)
         nc.sync.dma_start(w1_raw[:].bitcast(I32), w1_words[0].bitcast(I32))
-        n3_sb = load_list("n3_sb", n3, J)
+        cand_sb = load_list("cand_sb", cand, C)
         load_scale_rows(nc.sync, x_scale_table, x_scales, range(4))
         x_word_table = sb.tile([P, T], U32, align_bytes=64)
         nc.sync.dma_start(x_word_table[:].bitcast(I32), x_words[0].rearrange("p n r -> p (n r)").bitcast(I32))
         load_scale_rows(nc.sync, w1_scales_raw, w1_scales, range(4))
-        cand_sb = load_list("cand_sb", cand, C)
+        n3_sb = load_list("n3_sb", n3, J)
+        w2_raw = sb.tile([P, 2 * N], U8, align_bytes=64)
+        nc.sync.dma_start(w2_raw[:].bitcast(I32), w2_words[0].bitcast(I32))
         gs_sb = sb.tile([P, PACK], F32)
         nc.sync.dma_start(gs_sb[:], gs.rearrange("(p t) o -> p (t o)", t=PACK))
         n2_sb = load_list("n2_sb", n2, W)
         n1_sb = load_list("n1_sb", n1, W)
-        w2_raw = sb.tile([P, 2 * N], U8, align_bytes=64)
-        nc.sync.dma_start(w2_raw[:].bitcast(I32), w2_words[0].bitcast(I32))
         load_scale_rows(nc.sync, w2_scales_raw, w2_scales, range(4))
         gn_sb = sb.tile([P, PACK], F32)
         nc.sync.dma_start(gn_sb[:], gn.rearrange("(p t) o -> p (t o)", t=PACK))
@@ -101,6 +101,7 @@ def tile_picked_fkcdmaxbkmaxgpair_none_po_kernel(
         cand_plane_raw = sb.tile([P, C], U8, align_bytes=64)
         w1_codes = deal_words("w1_codes", w1_raw)
         nc.vector.tensor_copy(picked_plane[:], x_scale_table[:].indirect(offs_sb[:]))
+        nc.vector.tensor_copy(cand_plane_raw[:], x_scale_table[:].indirect(cand_sb[:]))
         nc.vector.tensor_copy(picked_codes[:], x_word_table[:].indirect(offs_sb[:]))
         w1_plane = sb.tile([P, H], U8, align_bytes=64)
         nc.vector.tensor_copy(w1_plane[:, :P], w1_scales_raw[:, 0:H:PACK])
@@ -128,9 +129,8 @@ def tile_picked_fkcdmaxbkmaxgpair_none_po_kernel(
         spread = sb.tile([P, PACK, S], F32, align_bytes=64)
         pa = sb.tile([P, PACK, W], F32, align_bytes=64)
         old = sb.tile([P, PACK, W], F32, align_bytes=64)
-        ra = sb.tile([P, PACK, W], F32, align_bytes=64)
-        z_bf = sb.tile([P, S, PACK], BF16, align_bytes=64)
-        z2_bf = sb.tile([P, S, PACK], BF16, align_bytes=64)
+        ra = []
+        z2_bf = sb.tile([P, S, PACK], BF16, tag="z2_then_ra", align_bytes=64)
 
         whole = slice(0, S)
         halves = (slice(0, S // 2), slice(S // 2, S))
@@ -154,16 +154,19 @@ def tile_picked_fkcdmaxbkmaxgpair_none_po_kernel(
             nc.scalar.activation(pa[:, t, :], y[t][:].indirect(n2_sb[:]), COPY)
             nc.scalar.activation(old[:, t, :], y[t][:].indirect(n1_sb[:]), COPY)
 
-        def take_ra(u):
+        def take_ra(u, tag):
             two = slice(2 * u, 2 * u + 2)
-            nc.vector.scalar_tensor_tensor(ra[:, two, :], old[:, two, :], 0.5, pa[:, two, :], ALU.mult, ALU.max)
+            ra.append(sb.tile([P, 2, W], F32, name="ra%d" % u, tag=tag, align_bytes=64))
+            nc.vector.scalar_tensor_tensor(ra[u][:], old[:, two, :], 0.5, pa[:, two, :], ALU.mult, ALU.max)
 
         def put(t):
-            nc.scalar.activation(y[t][:].indirect(n1_sb[:]), ra[:, t, :], COPY)
+            nc.scalar.activation(y[t][:].indirect(n1_sb[:]), ra[t // 2][:, t % 2, :], COPY)
 
         def round_z(t, cols):
             nc.vector.tensor_scalar(z_bf[:, cols, t], y[t][:, cols], gn_sb[:, t : t + 1], None, ALU.mult)
 
+        cand_plane = deal_scales("cand_plane", cand_plane_raw, "scale_rows")
+        w2_codes = deal_words("w2_codes", w2_raw)
         nc.scalar.activation(y[0][:, :S], y_psum[0][:], COPY)
         fetch_members(0)
         for t in range(1, PACK):
@@ -171,9 +174,8 @@ def tile_picked_fkcdmaxbkmaxgpair_none_po_kernel(
             fetch_members(t)
         for t in range(PACK):
             fetch_pair(t)
-        nc.vector.tensor_copy(cand_plane_raw[:], x_scale_table[:].indirect(cand_sb[:]))
         take_top(0)
-        cand_plane = deal_scales("cand_plane", cand_plane_raw)
+        w2_plane = deal_scales("w2_plane", w2_scales_raw, "w2_plane")
         take_gap(0)
         take_top(1)
         take_spread(0)
@@ -181,25 +183,23 @@ def tile_picked_fkcdmaxbkmaxgpair_none_po_kernel(
         take_top(2)
         take_spread(1)
         take_gap(2)
-        w2_codes = deal_words("w2_codes", w2_raw)
         take_top(3)
         take_spread(2)
         take_gap(3)
-        w2_plane = deal_scales("w2_plane", w2_scales_raw)
+        cand_codes = sb.tile([P, C], U32, tag="gathered_words", align_bytes=64)
+        nc.vector.tensor_copy(cand_codes[:].rearrange("p (t m) -> p m t", t=PACK), x_word_table[:].indirect(cand_sb[:]))
         take_spread(3)
-        take_ra(0)
         nc.vector.tensor_tensor(
             z2_bf[:].rearrange("p (c i) t -> p c t i", i=4),
             spread[:].rearrange("p t (c i) -> p c t i", i=4),
             gs_sb[:].rearrange("p (c t i) -> p c t i", c=1, i=1).to_broadcast([P, S // 4, PACK, 4]),
             ALU.mult,
         )
-        take_ra(1)
+        take_ra(0, "ra0")
+        z2_codes, z2_plane = quantise("z2", z2_bf)
+        take_ra(1, "z2_then_ra")
         for t in range(PACK):
             put(t)
-        z2_codes, z2_plane = quantise("z2", z2_bf)
-        cand_codes = sb.tile([P, C], U32, tag="gathered_words", align_bytes=64)
-        nc.vector.tensor_copy(cand_codes[:].rearrange("p (t m) -> p m t", t=PACK), x_word_table[:].indirect(cand_sb[:]))
         b_psum = [psum.tile([P, S], F32, name="b_psum%d" % t) for t in range(PACK)]
         for t in range(PACK):
             nc.tensor.matmul_mx(
@@ -211,10 +211,11 @@ def tile_picked_fkcdmaxbkmaxgpair_none_po_kernel(
                 start=True,
                 stop=True,
             )
-        round_z(0, whole)
-        round_z(1, whole)
         for t in range(PACK):
             nc.vector.tensor_scalar(b_win[t][:, :S], b_psum[t][:], 0.0625, None, ALU.mult)
+        z_bf = sb.tile([P, S, PACK], BF16, tag="gathered_words", align_bytes=64)
+        round_z(0, whole)
+        round_z(1, whole)
         round_z(2, whole)
         z_codes = sb.tile([P, S], U32, align_bytes=64)
         z_plane = sb.tile([P, S], U8, align_bytes=64)

@@ -41,7 +41,7 @@ def tile_picked_fkcdmaxbkmaxgpair_none_po_kernel(
                 queue.dma_start(plane[32 * q : 32 * q + 4, :].bitcast(I32), dram[0, 4 * q : 4 * q + 4, :].bitcast(I32))
 
         def deal_words(name, words):
-            dealt = sb.tile([P, 2 * H], U8, name=name, align_bytes=64)
+            dealt = sb.tile([P, 2 * H], U8, name=name, tag="weight_words", align_bytes=64)
             nc.vector.tensor_copy(
                 dealt[:].rearrange("p (t m b) -> p t m b", t=PACK, b=2),
                 words[:].rearrange("p (m t b) -> p t m b", t=PACK, b=2),
@@ -98,10 +98,10 @@ def tile_picked_fkcdmaxbkmaxgpair_none_po_kernel(
 
         picked_plane = sb.tile([P, S], U8, align_bytes=64)
         picked_codes = sb.tile([P, S], U32, tag="gathered_words", align_bytes=64)
-        cand_plane_raw = sb.tile([P, C], U8, align_bytes=64)
+        cand_rows = [sb.tile([P, C // 2], U8, name="cand_rows0", align_bytes=64)]
         w1_codes = deal_words("w1_codes", w1_raw)
         nc.vector.tensor_copy(picked_plane[:], x_scale_table[:].indirect(offs_sb[:]))
-        nc.vector.tensor_copy(cand_plane_raw[:], x_scale_table[:].indirect(cand_sb[:]))
+        nc.vector.tensor_copy(cand_rows[0][:], x_scale_table[:].indirect(cand_sb[:, : C // 32]))
         nc.vector.tensor_copy(picked_codes[:], x_word_table[:].indirect(offs_sb[:]))
         w1_plane = sb.tile([P, H], U8, align_bytes=64)
         nc.vector.tensor_copy(w1_plane[:, :P], w1_scales_raw[:, 0:H:PACK])
@@ -165,8 +165,8 @@ def tile_picked_fkcdmaxbkmaxgpair_none_po_kernel(
         def round_z(t, cols):
             nc.vector.tensor_scalar(z_bf[:, cols, t], y[t][:, cols], gn_sb[:, t : t + 1], None, ALU.mult)
 
-        cand_plane = deal_scales("cand_plane", cand_plane_raw, "scale_rows")
-        w2_codes = deal_words("w2_codes", w2_raw)
+        cand_rows.append(sb.tile([P, C // 2], U8, name="cand_rows1", tag="scale_rows", align_bytes=64))
+        nc.vector.tensor_copy(cand_rows[1][:], x_scale_table[:].indirect(cand_sb[:, C // 32 :]))
         nc.scalar.activation(y[0][:, :S], y_psum[0][:], COPY)
         fetch_members(0)
         for t in range(1, PACK):
@@ -174,12 +174,18 @@ def tile_picked_fkcdmaxbkmaxgpair_none_po_kernel(
             fetch_members(t)
         for t in range(PACK):
             fetch_pair(t)
+        w2_codes = deal_words("w2_codes", w2_raw)
         take_top(0)
-        w2_plane = deal_scales("w2_plane", w2_scales_raw, "w2_plane")
+        cand_plane = sb.tile([P, PACK, P], U8, align_bytes=64)
+        for u in range(2):
+            nc.vector.tensor_copy(
+                cand_plane[:, :, 64 * u : 64 * (u + 1)], cand_rows[u][:].rearrange("p (m t) -> p t m", t=PACK)
+            )
         take_gap(0)
         take_top(1)
         take_spread(0)
         take_gap(1)
+        w2_plane = deal_scales("w2_plane", w2_scales_raw, "w2_plane")
         take_top(2)
         take_spread(1)
         take_gap(2)
@@ -205,7 +211,7 @@ def tile_picked_fkcdmaxbkmaxgpair_none_po_kernel(
             nc.tensor.matmul_mx(
                 out=b_psum[t][:],
                 lhsT=cand_codes[:, P * t : P * (t + 1)].bitcast(FP8X4),
-                lhsT_scale=cand_plane[:, P * t : P * (t + 1)],
+                lhsT_scale=cand_plane[:, t, :],
                 rhs=z2_codes[:].bitcast(FP8X4),
                 rhs_scale=z2_plane[:],
                 start=True,

from contextlib import ExitStack

import concourse.mybir as mybir

K, T, S, N, H, W, J, C = 512, 2048, 256, 512, 512, 192, 512, 512
FLOPS = 2 * K * H * S + 2 * H * N * S + 2 * K * C * S

F32 = mybir.dt.float32
BF16 = mybir.dt.bfloat16
I32 = mybir.dt.int32
U32 = mybir.dt.uint32
U16 = mybir.dt.uint16
U8 = mybir.dt.uint8
FP8X4 = mybir.dt.float8_e4m3fn_x4
FP4X4 = mybir.dt.float4_e2m1fn_x4
ALU = mybir.AluOpType
COPY = mybir.ActivationFunctionType.Copy

P = 128
PACK = 4
Y_COLS = J + 16
AB_COLS = 2 * S


def tile_picked_fkcdmaxbkmaxgpair_none_po_kernel(
    tc, x_words, x_scales, w1_words, w1_scales, gn, w2_words, w2_scales, gs, offs, n1, n2, n3, cand, n4, n5, out_0, out_1, out_2
):
    nc = tc.nc
    with ExitStack() as ctx:
        lists = ctx.enter_context(tc.tile_pool(name="lists", bufs=1))
        sb = ctx.enter_context(tc.tile_pool(name="sb", bufs=1))
        psum = ctx.enter_context(tc.psum_pool(name="psum", bufs=1))

        def load_list(name, dram, entries):
            held = lists.tile([P, entries // 16], U16, name=name)
            nc.sync.dma_start(held[:], dram)
            return held

        def load_scale_rows(queue, plane, dram, quadrants):
            for q in quadrants:
                queue.dma_start(plane[32 * q : 32 * q + 4, :].bitcast(I32), dram[0, 4 * q : 4 * q + 4, :].bitcast(I32))

        def deal_words(name, words):
            dealt = sb.tile([P, 2 * H], U8, name=name, tag="weight_words", align_bytes=64)
            nc.vector.tensor_copy(
                dealt[:].rearrange("p (t m b) -> p t m b", t=PACK, b=2),
                words[:].rearrange("p (m t b) -> p t m b", t=PACK, b=2),
            )
            return dealt

        def deal_scales(name, scales, tag):
            dealt = sb.tile([P, H], U8, name=name, tag=tag, align_bytes=64)
            nc.vector.tensor_copy(
                dealt[:].rearrange("p (t m) -> p t m", t=PACK), scales[:].rearrange("p (m t) -> p t m", t=PACK)
            )
            return dealt

        def quantise(name, values):
            codes = sb.tile([P, S], U32, name=name + "_codes", align_bytes=64)
            plane = sb.tile([P, S], U8, name=name + "_plane", align_bytes=64)
            nc.vector.quantize_mx(out=codes[:].bitcast(FP8X4), scales=plane[:], in_=values[:].rearrange("p j t -> p (j t)"))
            return codes, plane

        def planes(name, cols):
            return [sb.tile([P, cols], F32, name="%s%d" % (name, t), align_bytes=64) for t in range(PACK)]

        x_scale_table = sb.tile([P, T], U8, align_bytes=64)
        w1_scales_raw = sb.tile([P, H], U8, tag="scale_rows", align_bytes=64)
        w2_scales_raw = sb.tile([P, N], U8, align_bytes=64)
        nc.vector.memset(x_scale_table[:, : T // 2].bitcast(I32), 0)
        nc.gpsimd.memset(x_scale_table[:, T // 2 :].bitcast(I32), 0)
        nc.vector.memset(w1_scales_raw[:].bitcast(I32), 0)
        nc.vector.memset(w2_scales_raw[:].bitcast(I32), 0)
        y = [sb.tile([P, Y_COLS], F32, name="y%d" % t, align_bytes=64) for t in range(PACK)]
        for t in range(PACK):
            nc.vector.memset(y[t][:, S:], 0.0)

        offs_sb = load_list("offs_sb", offs, S)
        w1_raw = sb.tile([P, 2 * H], U8, align_bytes=64)
        nc.sync.dma_start(w1_raw[:].bitcast(I32), w1_words[0].bitcast(I32))
        cand_sb = load_list("cand_sb", cand, C)
        load_scale_rows(nc.sync, x_scale_table, x_scales, range(4))
        x_word_table = sb.tile([P, T], U32, align_bytes=64)
        nc.sync.dma_start(x_word_table[:].bitcast(I32), x_words[0].rearrange("p n r -> p (n r)").bitcast(I32))
        load_scale_rows(nc.sync, w1_scales_raw, w1_scales, range(4))
        n3_sb = load_list("n3_sb", n3, J)
        w2_raw = sb.tile([P, 2 * N], U8, align_bytes=64)
        nc.sync.dma_start(w2_raw[:].bitcast(I32), w2_words[0].bitcast(I32))
        gs_sb = sb.tile([P, PACK], F32)
        nc.sync.dma_start(gs_sb[:], gs.rearrange("(p t) o -> p (t o)", t=PACK))
        n2_sb = load_list("n2_sb", n2, W)
        n1_sb = load_list("n1_sb", n1, W)
        load_scale_rows(nc.sync, w2_scales_raw, w2_scales, range(4))
        gn_sb = sb.tile([P, PACK], F32)
        nc.sync.dma_start(gn_sb[:], gn.rearrange("(p t) o -> p (t o)", t=PACK))
        n5_sb = load_list("n5_sb", n5, S)
        n4_sb = load_list("n4_sb", n4, S)

        picked_plane = sb.tile([P, S], U8, align_bytes=64)
        picked_codes = sb.tile([P, S], U32, tag="gathered_words", align_bytes=64)
        cand_rows = [sb.tile([P, C // 2], U8, name="cand_rows0", align_bytes=64)]
        w1_codes = deal_words("w1_codes", w1_raw)
        nc.vector.tensor_copy(picked_plane[:], x_scale_table[:].indirect(offs_sb[:]))
        nc.vector.tensor_copy(cand_rows[0][:], x_scale_table[:].indirect(cand_sb[:, : C // 32]))
        nc.vector.tensor_copy(picked_codes[:], x_word_table[:].indirect(offs_sb[:]))
        w1_plane = sb.tile([P, H], U8, align_bytes=64)
        nc.vector.tensor_copy(w1_plane[:, :P], w1_scales_raw[:, 0:H:PACK])
        nc.vector.tensor_copy(
            w1_plane[:, P:].rearrange("p (t m) -> p t m", t=PACK - 1),
            w1_scales_raw[:].rearrange("p (m t) -> p t m", t=PACK)[:, 1:, :],
        )

        y_psum = [psum.tile([P, S], F32, name="y_psum%d" % t, tag="ya%d" % t) for t in range(PACK)]
        for t in range(PACK):
            nc.tensor.matmul_mx(
                out=y_psum[t][:],
                lhsT=w1_codes[:, 2 * P * t : 2 * P * (t + 1)].bitcast(FP4X4),
                lhsT_scale=w1_plane[:, P * t : P * (t + 1)],
                rhs=picked_codes[:].bitcast(FP8X4),
                rhs_scale=picked_plane[:],
                start=True,
                stop=True,
            )

        a_win = planes("a_win", AB_COLS)
        b_win = planes("b_win", AB_COLS)
        members = planes("members", J)
        top = planes("top", S)
        spread = sb.tile([P, PACK, S], F32, align_bytes=64)
        pa = sb.tile([P, PACK, W], F32, align_bytes=64)
        old = sb.tile([P, PACK, W], F32, align_bytes=64)
        ra = []
        z2_bf = sb.tile([P, S, PACK], BF16, tag="z2_then_ra", align_bytes=64)

        whole = slice(0, S)
        halves = (slice(0, S // 2), slice(S // 2, S))

        def copy_y(t):
            nc.vector.tensor_copy(y[t][:, :S], y_psum[t][:])

        def fetch_members(t):
            nc.scalar.activation(members[t][:], y[t][:].indirect(n3_sb[:]), COPY)

        def take_top(t):
            nc.vector.tensor_tensor(top[t][:], y_psum[t][:], members[t][:, 0:J:2], ALU.max)

        def take_gap(t):
            nc.vector.tensor_tensor(b_win[t][:, S:], members[t][:, 1:J:2], top[t][:], ALU.subtract)

        def take_spread(t):
            nc.vector.scalar_tensor_tensor(spread[:, t, :], b_win[t][:, S:], 0.0, members[t][:, 0:J:2], ALU.min, ALU.add)

        def fetch_pair(t):
            nc.scalar.activation(pa[:, t, :], y[t][:].indirect(n2_sb[:]), COPY)
            nc.scalar.activation(old[:, t, :], y[t][:].indirect(n1_sb[:]), COPY)

        def take_ra(u, tag):
            two = slice(2 * u, 2 * u + 2)
            ra.append(sb.tile([P, 2, W], F32, name="ra%d" % u, tag=tag, align_bytes=64))
            nc.vector.scalar_tensor_tensor(ra[u][:], old[:, two, :], 0.5, pa[:, two, :], ALU.mult, ALU.max)

        def put(t):
            nc.scalar.activation(y[t][:].indirect(n1_sb[:]), ra[t // 2][:, t % 2, :], COPY)

        def round_z(t, cols):
            nc.vector.tensor_scalar(z_bf[:, cols, t], y[t][:, cols], gn_sb[:, t : t + 1], None, ALU.mult)

        cand_rows.append(sb.tile([P, C // 2], U8, name="cand_rows1", tag="scale_rows", align_bytes=64))
        nc.vector.tensor_copy(cand_rows[1][:], x_scale_table[:].indirect(cand_sb[:, C // 32 :]))
        nc.scalar.activation(y[0][:, :S], y_psum[0][:], COPY)
        fetch_members(0)
        for t in range(1, PACK):
            copy_y(t)
            fetch_members(t)
        for t in range(PACK):
            fetch_pair(t)
        w2_codes = deal_words("w2_codes", w2_raw)
        take_top(0)
        cand_plane = sb.tile([P, PACK, P], U8, align_bytes=64)
        for u in range(2):
            nc.vector.tensor_copy(
                cand_plane[:, :, 64 * u : 64 * (u + 1)], cand_rows[u][:].rearrange("p (m t) -> p t m", t=PACK)
            )
        take_gap(0)
        take_top(1)
        take_spread(0)
        take_gap(1)
        w2_plane = deal_scales("w2_plane", w2_scales_raw, "w2_plane")
        take_top(2)
        take_spread(1)
        take_gap(2)
        take_top(3)
        take_spread(2)
        take_gap(3)
        cand_codes = sb.tile([P, C], U32, tag="gathered_words", align_bytes=64)
        nc.vector.tensor_copy(cand_codes[:].rearrange("p (t m) -> p m t", t=PACK), x_word_table[:].indirect(cand_sb[:]))
        take_spread(3)
        nc.vector.tensor_tensor(
            z2_bf[:].rearrange("p (c i) t -> p c t i", i=4),
            spread[:].rearrange("p t (c i) -> p c t i", i=4),
            gs_sb[:].rearrange("p (c t i) -> p c t i", c=1, i=1).to_broadcast([P, S // 4, PACK, 4]),
            ALU.mult,
        )
        take_ra(0, "ra0")
        z2_codes, z2_plane = quantise("z2", z2_bf)
        take_ra(1, "z2_then_ra")
        for t in range(PACK):
            put(t)
        b_psum = [psum.tile([P, S], F32, name="b_psum%d" % t) for t in range(PACK)]
        for t in range(PACK):
            nc.tensor.matmul_mx(
                out=b_psum[t][:],
                lhsT=cand_codes[:, P * t : P * (t + 1)].bitcast(FP8X4),
                lhsT_scale=cand_plane[:, t, :],
                rhs=z2_codes[:].bitcast(FP8X4),
                rhs_scale=z2_plane[:],
                start=True,
                stop=True,
            )
        for t in range(PACK):
            nc.vector.tensor_scalar(b_win[t][:, :S], b_psum[t][:], 0.0625, None, ALU.mult)
        z_bf = sb.tile([P, S, PACK], BF16, tag="gathered_words", align_bytes=64)
        round_z(0, whole)
        round_z(1, whole)
        round_z(2, whole)
        z_codes = sb.tile([P, S], U32, align_bytes=64)
        z_plane = sb.tile([P, S], U8, align_bytes=64)
        for cols in halves:
            round_z(3, cols)
        for cols in halves:
            nc.vector.quantize_mx(
                out=z_codes[:, cols].bitcast(FP8X4),
                scales=z_plane[:, cols],
                in_=z_bf[:, cols, :].rearrange("p j t -> p (j t)"),
            )
        a_psum = [psum.tile([P, S], F32, name="a_psum%d" % t, tag="ya%d" % t) for t in range(PACK)]
        for t in range(PACK):
            nc.tensor.matmul_mx(
                out=a_psum[t][:],
                lhsT=w2_codes[:, 2 * P * t : 2 * P * (t + 1)].bitcast(FP4X4),
                lhsT_scale=w2_plane[:, P * t : P * (t + 1)],
                rhs=z_codes[:].bitcast(FP8X4),
                rhs_scale=z_plane[:],
                start=True,
                stop=True,
            )

        for t in range(PACK):
            nc.scalar.activation(a_win[t][:, S:], b_win[t][:].indirect(n5_sb[:]), COPY)
        for t in range(PACK):
            nc.vector.tensor_copy(a_win[t][:, :S], a_psum[t][:])

        result = sb.tile([P, PACK, S], F32, align_bytes=64)
        result_bf = sb.tile([P, S, PACK], BF16, align_bytes=64)
        out_rows = out_0.rearrange("(p t) j -> p t j", t=PACK)
        high = planes("high", S)
        low = planes("low", S)
        a_at = planes("a_at", S)

        out_codes = sb.tile([P, S], U32, align_bytes=64)
        out_plane = sb.tile([P, S], U8, align_bytes=64)

        def fetch_a(t, cols):
            nc.scalar.activation(a_at[t][:, cols], a_win[t][:].indirect(n4_sb[:, cols.start // 16 : cols.stop // 16]), COPY)

        def take_high(t):
            nc.vector.tensor_tensor(high[t][:], a_psum[t][:], a_win[t][:, S:], ALU.max)

        def take_low(t, cols):
            nc.vector.scalar_tensor_tensor(low[t][:, cols], b_psum[t][:, cols], 0.0625, a_at[t][:, cols], ALU.mult, ALU.min)

        def take_result(engine, t, cols):
            engine.tensor_tensor(result[:, t, cols], high[t][:, cols], low[t][:, cols], ALU.subtract)

        def round_result(cols):
            nc.vector.tensor_copy(
                result_bf[:, cols, :].rearrange("p (c i) t -> p c t i", i=4),
                result[:, :, cols].rearrange("p t (c i) -> p c t i", i=4),
            )

        def quantise_result(cols):
            nc.vector.quantize_mx(
                out=out_codes[:, cols].bitcast(FP8X4),
                scales=out_plane[:, cols],
                in_=result_bf[:, cols, :].rearrange("p j t -> p (j t)"),
            )

        for t in range(PACK - 1):
            fetch_a(t, whole)
        for cols in halves:
            fetch_a(PACK - 1, cols)
        take_high(0)
        take_high(1)
        take_low(0, whole)
        take_high(2)
        take_low(1, whole)
        take_result(nc.gpsimd, 0, whole)
        take_high(3)
        take_result(nc.gpsimd, 1, whole)
        nc.sync.dma_start(out_rows[:, 0:2, :], result[:, 0:2, :])
        take_low(2, whole)
        for cols in halves:
            take_low(3, cols)
        take_result(nc.vector, 2, whole)
        for cols in halves:
            take_result(nc.vector, 3, cols)
        nc.sync.dma_start(out_rows[:, 2:4, :], result[:, 2:4, :])
        for cols in halves:
            round_result(cols)
        for cols in halves:
            quantise_result(cols)
        nc.sync.dma_start(out_1[0].rearrange("p n r -> p (n r)").bitcast(I32), out_codes[:].bitcast(I32))
        for q in range(4):
            queue = nc.scalar if q % 2 == 0 else nc.sync
            queue.dma_start(out_2[0, 4 * q : 4 * q + 4, :].bitcast(I32), out_plane[32 * q : 32 * q + 4, :].bitcast(I32))
